import numpy as np
import ml_dtypes


def mxq(x, axis, fmt="e4m3"):
    dtype, down = {"e4m3": (ml_dtypes.float8_e4m3fn, 7), "e5m2": (ml_dtypes.float8_e5m2, 14)}[fmt]
    v = np.moveaxis(np.asarray(x, np.float32).astype(ml_dtypes.bfloat16).astype(np.float64), axis, -1)
    blocks = v.reshape(v.shape[:-1] + (-1, 32))
    amax = np.abs(blocks).max(-1, keepdims=True)
    byte = np.maximum(np.where(amax > 0, np.frexp(amax)[1] - 1 + 127, 0) - down, 1)
    scale = np.exp2(byte - 127.0)
    codes = (blocks / scale).astype(np.float32).astype(dtype).astype(np.float64)
    return np.moveaxis((codes * scale).reshape(v.shape), -1, axis)


WIDE = False


def mx_kscale(k):
    if not WIDE:
        return np.ones(k)
    levels = np.array([10, -10, 5, -5, 0])
    if k % 512:
        return np.exp2(np.random.permutation(np.resize(levels, k // 32))).repeat(32)
    a = np.empty((k // 512, 16))
    for p in range(k // 512):
        a[p, :8] = np.random.permutation(np.resize(levels, 8))
        for g in range(8):
            far = levels[np.abs(levels - a[p, g]) >= 10]
            a[p, g + 8] = far[np.random.randint(len(far))]
    return np.exp2(a.ravel()).repeat(32)


def f64(x):
    return np.asarray(x).astype(np.float64)


def striped8(idx):
    return np.asarray(idx).reshape(8, -1, 16).transpose(0, 2, 1).reshape(128, -1).astype(np.uint16)


def unstriped8(offs):
    return offs.reshape(8, 16, -1).transpose(0, 2, 1).reshape(8, -1).astype(np.int64)


def pick8(x, idx, run):
    r = np.arange(len(x))
    return x[r[:, None], idx[r % (8 * run) // run]]


E2M1 = np.array([0.0, 0.5, 1.0, 1.5, 2.0, 3.0, 4.0, 6.0, -0.0, -0.5, -1.0, -1.5, -2.0, -3.0, -4.0, -6.0])


def pack_weight(w, fmt):
    k, n = w.shape
    w = f64(np.asarray(w, np.float32).astype(ml_dtypes.bfloat16)).reshape(k // 32, 32, n)
    amax = np.abs(w).max(1)
    if fmt == "e4m3":
        byte = np.frexp(amax)[1] - 1 + 127 - 7
    else:
        mant, ex = np.frexp(amax / 6.0)
        byte = np.where(mant > 0.5, ex, ex - 1) + 127
    byte = np.clip(np.where(amax > 0, byte, 1), 1, 254)
    scaled = (w * np.exp2(127.0 - byte)[:, None, :]).reshape(k, n).astype(np.float32)
    by_word = np.ascontiguousarray(scaled.reshape(k // 512, 128, 4, n).transpose(0, 1, 3, 2))
    if fmt == "e4m3":
        words = by_word.astype(ml_dtypes.float8_e4m3fn).view(np.uint8)
    else:
        c = by_word.astype(ml_dtypes.float4_e2m1fn).view(np.uint8) & 0xF
        words = (c[..., 0::2] | (c[..., 1::2] << 4)).reshape(k // 512, 128, 2 * n)
    return np.ascontiguousarray(words), np.ascontiguousarray(byte.astype(np.uint8).reshape(k // 512, 16, n))


def unpack_weight(words, scales, fmt):
    g, _, n = scales.shape
    words = np.ascontiguousarray(words).reshape(g, 128, n, -1)
    if fmt == "e4m3":
        vals = words.view(ml_dtypes.float8_e4m3fn).astype(np.float64)
    else:
        nib = np.empty((g, 128, n, 4), np.uint8)
        nib[..., 0::2] = words & 0xF
        nib[..., 1::2] = words >> 4
        vals = E2M1[nib]
    vals = vals * np.repeat(np.exp2(scales.astype(np.float64) - 127.0), 8, axis=1)[..., None]
    return vals.transpose(0, 1, 3, 2).reshape(g * 512, n)


D, T, I, Q = 512, 1024, 512, 128


def setup_inputs():
    n = np.random.standard_normal
    idx = np.stack([np.random.permutation(T)[:I] for _ in range(8)])
    idx2 = np.stack([np.random.permutation(T)[:I] for _ in range(8)])
    idx3 = np.stack([np.random.permutation(T)[:I] for _ in range(8)])
    fd = mx_kscale(D)
    keysp = pack_weight(n((D, T)) / fd[:, None], "e4m3")
    return {
        "query": (n((D, Q)) * 1.0 / np.sqrt(D) * fd[:, None]).astype(np.float32),
        "keys_words": keysp[0],
        "keys_scales": keysp[1],
        "lam": (np.random.uniform(0.4, 1.0, (Q, 1))).astype(np.float32),
        "pull": (np.random.uniform(0.3, 0.9, (Q, 1))).astype(np.float32),
        "old": (np.random.uniform(0.0, 2.0, (Q, T))).astype(np.float32),
        "fade": (np.random.uniform(0.3, 0.9, (Q, 1))).astype(np.float32),
        "offs": striped8(idx),
        "offs2": striped8(idx2),
        "offs3": striped8(idx3),
    }


def reference(query, keys_words, keys_scales, lam, pull, old, fade, offs, offs2, offs3):
    idx = unstriped8(offs)
    idx2 = unstriped8(offs2)
    idx3 = unstriped8(offs3)
    keysu = unpack_weight(keys_words, keys_scales, "e4m3")
    queryq = mxq(f64(query), 0, "e4m3")
    a = queryq.T @ keysu
    s = pick8(a, idx, 16) + np.tanh(pick8(a, idx2, 16) - pick8(a, idx3, 16)) * f64(lam)
    p = np.exp(s - np.max(s, axis=1, keepdims=True))
    r = p / np.sum(p, axis=1, keepdims=True)
    r1 = np.pad(r, ((0, 0), (1, 0)))[:, :I]
    w = r - r1 * f64(pull)
    ws = w * 256.0
    wf = np.zeros((Q, T))
    wf[np.arange(Q)[:, None], idx[np.arange(Q) % 128 // 16]] = ws
    y = f64(old) * f64(fade) + wf
    return y

@@ -1,0 +1,213 @@
+from contextlib import ExitStack
+
+import concourse.mybir as mybir
+
+D, T, I, Q = 512, 1024, 512, 128
+FLOPS = 2 * D * T * Q
+
+F32 = mybir.dt.float32
+BF16 = mybir.dt.bfloat16
+I32 = mybir.dt.int32
+U32 = mybir.dt.uint32
+U16 = mybir.dt.uint16
+U8 = mybir.dt.uint8
+FP8X4 = mybir.dt.float8_e4m3fn_x4
+ALU = mybir.AluOpType
+ACT = mybir.ActivationFunctionType
+
+P = 128
+PACK = 4
+MM_COLS = 256
+HALF = I // 2
+LEAD = 8
+OUT_COLS = 256
+
+
+def tile_attend_seconded_stepwise_counts_heads_kernel(
+    tc, query, keys_words, keys_scales, lam, pull, old, fade, offs, offs2, offs3, out
+):
+    nc = tc.nc
+    with ExitStack() as ctx:
+        held = ctx.enter_context(tc.tile_pool(name="held", bufs=1))
+        psum = ctx.enter_context(tc.psum_pool(name="psum", bufs=1))
+
+        own_list = held.tile([P, I // 16], U16, name="own_list")
+        seconder_list = held.tile([P, I // 16], U16, name="seconder_list")
+        opponent_list = held.tile([P, I // 16], U16, name="opponent_list")
+
+        key_scales = held.tile([P, T], U8, name="key_scales", align_bytes=64)
+        nc.vector.memset(key_scales[:].bitcast(I32), 0)
+
+        q_raw = held.tile([P, PACK, Q], F32, name="q_raw", tag="q_then_old")
+        nc.sync.dma_start(out=q_raw[:], in_=query.rearrange("(p j) q -> p j q", j=PACK))
+        key_words = held.tile([P, T], U32, name="key_words", align_bytes=64)
+        nc.sync.dma_start(
+            out=key_words[:].bitcast(I32),
+            in_=keys_words[0].rearrange("p n t -> p (n t)").bitcast(I32),
+        )
+        for quad in range(4):
+            nc.scalar.dma_start(
+                out=key_scales[32 * quad : 32 * quad + 4, :].bitcast(I32),
+                in_=keys_scales[0, 4 * quad : 4 * quad + 4, :].bitcast(I32),
+            )
+        nc.sync.dma_start(opponent_list[:], offs3)
+        nc.sync.dma_start(seconder_list[:], offs2)
+        nc.sync.dma_start(own_list[:], offs)
+
+        lam_col = held.tile([P, 1], F32, name="lam_col")
+        pull_col = held.tile([P, 1], F32, name="pull_col")
+        fade_col = held.tile([P, 1], F32, name="fade_col")
+        nc.gpsimd.dma_start(out=lam_col[:], in_=lam)
+        nc.gpsimd.dma_start(out=pull_col[:], in_=pull)
+        nc.gpsimd.dma_start(out=fade_col[:], in_=fade)
+
+        placed = held.tile([P, T], F32, name="placed")
+        nc.vector.memset(placed[:], 0.0)
+        shares = held.tile([P, LEAD + I], F32, name="shares")
+        nc.vector.memset(shares[:, 0:LEAD], 0.0)
+
+        q_grouped = held.tile([P, Q, PACK], BF16, name="q_grouped", align_bytes=64)
+        nc.vector.tensor_copy(out=q_grouped[:], in_=q_raw[:].rearrange("p j q -> p q j"))
+        q_words = held.tile([P, Q], U32, name="q_words", align_bytes=64)
+        q_scales = held.tile([P, Q], U8, name="q_scales", align_bytes=64)
+        nc.vector.quantize_mx(
+            out=q_words[:].bitcast(FP8X4),
+            scales=q_scales[:],
+            in_=q_grouped[:].rearrange("p q j -> p (q j)"),
+        )
+
+        old_sb = held.tile([P, T], F32, name="old_sb", tag="q_then_old")
+        nc.sync.dma_start(out=old_sb[:], in_=old)
+
+        neg_pull = held.tile([P, 1], F32, name="neg_pull")
+        nc.gpsimd.tensor_scalar(
+            out=neg_pull[:], in0=pull_col[:], scalar1=-1.0, scalar2=0.0, op0=ALU.mult, op1=ALU.add
+        )
+
+        products = held.tile([P, T], F32, name="products")
+        for c in range(T // MM_COLS):
+            cols = slice(c * MM_COLS, (c + 1) * MM_COLS)
+            bank = psum.tile([P, MM_COLS], F32, name="bank%d" % c)
+            nc.tensor.matmul_mx(
+                out=bank[:],
+                lhsT=q_words[:].bitcast(FP8X4),
+                lhsT_scale=q_scales[:],
+                rhs=key_words[:, cols].bitcast(FP8X4),
+                rhs_scale=key_scales[:, cols],
+                start=True,
+                stop=True,
+            )
+            if c % 2 == 0:
+                nc.scalar.activation(out=products[:, cols], in_=bank[:], func=ACT.Copy)
+            else:
+                nc.vector.tensor_copy(out=products[:, cols], in_=bank[:])
+
+        slots = [slice(0, HALF), slice(HALF, I)]
+        entries = [slice(0, HALF // 16), slice(HALF // 16, I // 16)]
+
+        opponent = held.tile([P, I], F32, name="opponent")
+        own = held.tile([P, I], F32, name="own")
+        gap = held.tile([P, I], F32, name="gap")
+        vote = held.tile([P, I], F32, name="vote")
+        score = held.tile([P, I], F32, name="score")
+        neg_score = held.tile([P, I], F32, name="neg_score", tag="score_then_faded")
+        neg_top = [held.tile([P, 1], F32, name="neg_top%d" % h) for h in range(2)]
+
+        nc.vector.tensor_copy(out=own[:, slots[0]], in_=products[:].indirect(own_list[:, entries[0]]))
+        for h in range(2):
+            nc.scalar.activation(
+                out=opponent[:, slots[h]],
+                in_=products[:].indirect(opponent_list[:, entries[h]]),
+                func=ACT.Copy,
+            )
+        for h in range(2):
+            nc.vector.tensor_tensor(
+                out=gap[:, slots[h]],
+                in0=products[:].indirect(seconder_list[:, entries[h]]),
+                in1=opponent[:, slots[h]],
+                op=ALU.subtract,
+            )
+        nc.scalar.activation(out=vote[:, slots[0]], in_=gap[:, slots[0]], func=ACT.Tanh)
+        nc.scalar.activation(
+            out=own[:, slots[1]], in_=products[:].indirect(own_list[:, entries[1]]), func=ACT.Copy
+        )
+        nc.scalar.activation(out=vote[:, slots[1]], in_=gap[:, slots[1]], func=ACT.Tanh)
+        for h in range(2):
+            nc.vector.scalar_tensor_tensor(
+                out=score[:, slots[h]],
+                in0=vote[:, slots[h]],
+                scalar=lam_col[:],
+                in1=own[:, slots[h]],
+                op0=ALU.mult,
+                op1=ALU.add,
+            )
+            nc.vector.tensor_scalar(
+                out=neg_score[:, slots[h]],
+                in0=score[:, slots[h]],
+                scalar1=-1.0,
+                scalar2=None if h == 0 else neg_top[0][:],
+                op0=ALU.mult,
+                op1=ALU.min,
+                accum_out=neg_top[h][:],
+            )
+
+        part_sum = [held.tile([P, 1], F32, name="part_sum%d" % h) for h in range(2)]
+        pulled = held.tile([P, I], F32, name="pulled")
+        total = held.tile([P, 1], F32, name="total")
+        norm = held.tile([P, 1], F32, name="norm")
+        for h in range(2):
+            nc.scalar.activation(
+                out=shares[:, LEAD + h * HALF : LEAD + (h + 1) * HALF],
+                in_=neg_score[:, slots[h]],
+                func=ACT.Exp,
+                bias=neg_top[1][:],
+                scale=-1.0,
+                accum_out=part_sum[h][:],
+            )
+        nc.vector.tensor_scalar(
+            out=pulled[:, slots[0]],
+            in0=shares[:, LEAD - 1 : LEAD - 1 + HALF],
+            scalar1=neg_pull[:],
+            scalar2=None,
+            op0=ALU.mult,
+        )
+        nc.scalar.activation(
+            out=pulled[:, slots[1]],
+            in_=shares[:, LEAD - 1 + HALF : LEAD - 1 + I],
+            func=ACT.Copy,
+            scale=neg_pull[:],
+        )
+        faded = held.tile([P, T], F32, name="faded", tag="score_then_faded")
+        nc.scalar.activation(out=faded[:], in_=old_sb[:], func=ACT.Copy, scale=fade_col[:])
+
+        for h in range(2):
+            nc.vector.tensor_tensor(
+                out=placed[:].indirect(own_list[:, entries[h]]),
+                in0=shares[:, LEAD + h * HALF : LEAD + (h + 1) * HALF],
+                in1=pulled[:, slots[h]],
+                op=ALU.add,
+            )
+            if h == 0:
+                nc.vector.tensor_scalar(
+                    out=total[:],
+                    in0=part_sum[0][:],
+                    scalar1=part_sum[1][:],
+                    scalar2=1.0 / 256.0,
+                    op0=ALU.add,
+                    op1=ALU.mult,
+                )
+        nc.vector.reciprocal(out=norm[:], in_=total[:])
+
+        for c in range(T // OUT_COLS):
+            cols = slice(c * OUT_COLS, (c + 1) * OUT_COLS)
+            result = held.tile([P, OUT_COLS], F32, name="result%d" % c)
+            nc.vector.scalar_tensor_tensor(
+                out=result[:],
+                in0=placed[:, cols],
+                scalar=norm[:],
+                in1=faded[:, cols],
+                op0=ALU.mult,
+                op1=ALU.add,
+            )
+            queue = nc.sync if c % 2 == 0 else nc.scalar
+            queue.dma_start(out=out[:, cols], in_=result[:])

@@ -17,10 +17,11 @@ ACT = mybir.ActivationFunctionType
 
 P = 128
 PACK = 4
-MM_COLS = 256
+MM_WIDTHS = (256, 256, 256, 128, 128)
 HALF = I // 2
 LEAD = 8
-OUT_COLS = 256
+FIRST = 128
+OUT_WIDTHS = (256, 256, 256, 256)
 
 
 def tile_attend_seconded_stepwise_counts_heads_kernel(
@@ -36,20 +37,20 @@ def tile_attend_seconded_stepwise_counts_heads_kernel(
         opponent_list = held.tile([P, I // 16], U16, name="opponent_list")
 
         key_scales = held.tile([P, T], U8, name="key_scales", align_bytes=64)
-        nc.vector.memset(key_scales[:].bitcast(I32), 0)
 
-        q_raw = held.tile([P, PACK, Q], F32, name="q_raw", tag="q_then_old")
+        q_raw = held.tile([P, PACK, Q], F32, name="q_raw")
         nc.sync.dma_start(out=q_raw[:], in_=query.rearrange("(p j) q -> p j q", j=PACK))
-        key_words = held.tile([P, T], U32, name="key_words", align_bytes=64)
-        nc.sync.dma_start(
-            out=key_words[:].bitcast(I32),
-            in_=keys_words[0].rearrange("p n t -> p (n t)").bitcast(I32),
-        )
         for quad in range(4):
-            nc.scalar.dma_start(
+            queue = nc.sync if quad < 2 else nc.scalar
+            queue.dma_start(
                 out=key_scales[32 * quad : 32 * quad + 4, :].bitcast(I32),
                 in_=keys_scales[0, 4 * quad : 4 * quad + 4, :].bitcast(I32),
             )
+        key_words = held.tile([P, T], U32, name="key_words", align_bytes=64)
+        words_hbm = keys_words[0].rearrange("p n t -> p (n t)").bitcast(I32)
+        for c in range(2):
+            cols = slice(c * T // 2, (c + 1) * T // 2)
+            nc.sync.dma_start(out=key_words[:, cols].bitcast(I32), in_=words_hbm[:, cols])
         nc.sync.dma_start(opponent_list[:], offs3)
         nc.sync.dma_start(seconder_list[:], offs2)
         nc.sync.dma_start(own_list[:], offs)
@@ -57,9 +58,11 @@ def tile_attend_seconded_stepwise_counts_heads_kernel(
         lam_col = held.tile([P, 1], F32, name="lam_col")
         pull_col = held.tile([P, 1], F32, name="pull_col")
         fade_col = held.tile([P, 1], F32, name="fade_col")
-        nc.gpsimd.dma_start(out=lam_col[:], in_=lam)
-        nc.gpsimd.dma_start(out=pull_col[:], in_=pull)
-        nc.gpsimd.dma_start(out=fade_col[:], in_=fade)
+        nc.sync.dma_start(out=lam_col[:], in_=lam)
+        nc.sync.dma_start(out=pull_col[:], in_=pull)
+        nc.sync.dma_start(out=fade_col[:], in_=fade)
+        old_sb = held.tile([P, T], F32, name="old_sb")
+        nc.sync.dma_start(out=old_sb[:], in_=old)
 
         placed = held.tile([P, T], F32, name="placed")
         nc.vector.memset(placed[:], 0.0)
@@ -67,17 +70,19 @@ def tile_attend_seconded_stepwise_counts_heads_kernel(
         nc.vector.memset(shares[:, 0:LEAD], 0.0)
 
         q_grouped = held.tile([P, Q, PACK], BF16, name="q_grouped", align_bytes=64)
-        nc.vector.tensor_copy(out=q_grouped[:], in_=q_raw[:].rearrange("p j q -> p q j"))
+        q_halves = [slice(0, Q // 2), slice(Q // 2, Q)]
+        for rows in q_halves:
+            nc.vector.tensor_copy(
+                out=q_grouped[:, rows, :], in_=q_raw[:, :, rows].rearrange("p j q -> p q j")
+            )
         q_words = held.tile([P, Q], U32, name="q_words", align_bytes=64)
         q_scales = held.tile([P, Q], U8, name="q_scales", align_bytes=64)
-        nc.vector.quantize_mx(
-            out=q_words[:].bitcast(FP8X4),
-            scales=q_scales[:],
-            in_=q_grouped[:].rearrange("p q j -> p (q j)"),
-        )
-
-        old_sb = held.tile([P, T], F32, name="old_sb", tag="q_then_old")
-        nc.sync.dma_start(out=old_sb[:], in_=old)
+        for rows in q_halves:
+            nc.vector.quantize_mx(
+                out=q_words[:, rows].bitcast(FP8X4),
+                scales=q_scales[:, rows],
+                in_=q_grouped[:, rows, :].rearrange("p q j -> p (q j)"),
+            )
 
         neg_pull = held.tile([P, 1], F32, name="neg_pull")
         nc.gpsimd.tensor_scalar(
@@ -85,9 +90,9 @@ def tile_attend_seconded_stepwise_counts_heads_kernel(
         )
 
         products = held.tile([P, T], F32, name="products")
-        for c in range(T // MM_COLS):
-            cols = slice(c * MM_COLS, (c + 1) * MM_COLS)
-            bank = psum.tile([P, MM_COLS], F32, name="bank%d" % c)
+        for c, width in enumerate(MM_WIDTHS):
+            cols = slice(sum(MM_WIDTHS[:c]), sum(MM_WIDTHS[: c + 1]))
+            bank = psum.tile([P, width], F32, name="bank%d" % c)
             nc.tensor.matmul_mx(
                 out=bank[:],
                 lhsT=q_words[:].bitcast(FP8X4),
@@ -106,101 +111,99 @@ def tile_attend_seconded_stepwise_counts_heads_kernel(
         entries = [slice(0, HALF // 16), slice(HALF // 16, I // 16)]
 
         opponent = held.tile([P, I], F32, name="opponent")
-        own = held.tile([P, I], F32, name="own")
+        seconder = [
+            held.tile([P, HALF], F32, name="seconder0", tag="seconder_then_own"),
+            held.tile([P, HALF], F32, name="seconder1"),
+        ]
         gap = held.tile([P, I], F32, name="gap")
         vote = held.tile([P, I], F32, name="vote")
-        score = held.tile([P, I], F32, name="score")
-        neg_score = held.tile([P, I], F32, name="neg_score", tag="score_then_faded")
-        neg_top = [held.tile([P, 1], F32, name="neg_top%d" % h) for h in range(2)]
+        score = held.tile([P, I], F32, name="score", tag="score_then_faded")
+        neg_top = held.tile([P, 1], F32, name="neg_top")
 
-        nc.vector.tensor_copy(out=own[:, slots[0]], in_=products[:].indirect(own_list[:, entries[0]]))
         for h in range(2):
             nc.scalar.activation(
                 out=opponent[:, slots[h]],
                 in_=products[:].indirect(opponent_list[:, entries[h]]),
                 func=ACT.Copy,
             )
+            nc.vector.tensor_copy(
+                out=seconder[h][:], in_=products[:].indirect(seconder_list[:, entries[h]])
+            )
         for h in range(2):
             nc.vector.tensor_tensor(
-                out=gap[:, slots[h]],
-                in0=products[:].indirect(seconder_list[:, entries[h]]),
-                in1=opponent[:, slots[h]],
-                op=ALU.subtract,
+                out=gap[:, slots[h]], in0=seconder[h][:], in1=opponent[:, slots[h]], op=ALU.subtract
             )
-        nc.scalar.activation(out=vote[:, slots[0]], in_=gap[:, slots[0]], func=ACT.Tanh)
+        own = [
+            held.tile([P, HALF], F32, name="own0"),
+            held.tile([P, HALF], F32, name="own1", tag="seconder_then_own"),
+        ]
         nc.scalar.activation(
-            out=own[:, slots[1]], in_=products[:].indirect(own_list[:, entries[1]]), func=ACT.Copy
+            out=own[0][:], in_=products[:].indirect(own_list[:, entries[0]]), func=ACT.Copy
         )
-        nc.scalar.activation(out=vote[:, slots[1]], in_=gap[:, slots[1]], func=ACT.Tanh)
+        nc.vector.tensor_copy(out=own[1][:], in_=products[:].indirect(own_list[:, entries[1]]))
+        for h in range(2):
+            nc.scalar.activation(out=vote[:, slots[h]], in_=gap[:, slots[h]], func=ACT.Tanh)
         for h in range(2):
             nc.vector.scalar_tensor_tensor(
                 out=score[:, slots[h]],
                 in0=vote[:, slots[h]],
                 scalar=lam_col[:],
-                in1=own[:, slots[h]],
+                in1=own[h][:],
                 op0=ALU.mult,
                 op1=ALU.add,
             )
-            nc.vector.tensor_scalar(
-                out=neg_score[:, slots[h]],
-                in0=score[:, slots[h]],
-                scalar1=-1.0,
-                scalar2=None if h == 0 else neg_top[0][:],
-                op0=ALU.mult,
-                op1=ALU.min,
-                accum_out=neg_top[h][:],
-            )
+        nc.vector.tensor_reduce(
+            out=neg_top[:], in_=score[:], axis=mybir.AxisListType.X, op=ALU.max, negate=True
+        )
 
         part_sum = [held.tile([P, 1], F32, name="part_sum%d" % h) for h in range(2)]
-        pulled = held.tile([P, I], F32, name="pulled")
-        total = held.tile([P, 1], F32, name="total")
-        norm = held.tile([P, 1], F32, name="norm")
+        pieces = [slice(0, FIRST), slice(FIRST, I)]
         for h in range(2):
             nc.scalar.activation(
-                out=shares[:, LEAD + h * HALF : LEAD + (h + 1) * HALF],
-                in_=neg_score[:, slots[h]],
+                out=shares[:, LEAD + pieces[h].start : LEAD + pieces[h].stop],
+                in_=score[:, pieces[h]],
                 func=ACT.Exp,
-                bias=neg_top[1][:],
-                scale=-1.0,
+                bias=neg_top[:],
                 accum_out=part_sum[h][:],
             )
-        nc.vector.tensor_scalar(
-            out=pulled[:, slots[0]],
-            in0=shares[:, LEAD - 1 : LEAD - 1 + HALF],
-            scalar1=neg_pull[:],
-            scalar2=None,
+        first_weights = held.tile([P, FIRST], F32, name="first_weights")
+        nc.vector.scalar_tensor_tensor(
+            out=first_weights[:],
+            in0=shares[:, LEAD - 1 : LEAD - 1 + FIRST],
+            scalar=neg_pull[:],
+            in1=shares[:, LEAD : LEAD + FIRST],
             op0=ALU.mult,
+            op1=ALU.add,
         )
+        total = held.tile([P, 1], F32, name="total")
+        inverse = held.tile([P, 1], F32, name="inverse")
+        norm = held.tile([P, 1], F32, name="norm")
+        nc.scalar.activation(out=total[:], in_=part_sum[0][:], func=ACT.Identity, bias=part_sum[1][:])
+        pulled = held.tile([P, I - FIRST], F32, name="pulled")
         nc.scalar.activation(
-            out=pulled[:, slots[1]],
-            in_=shares[:, LEAD - 1 + HALF : LEAD - 1 + I],
+            out=pulled[:],
+            in_=shares[:, LEAD - 1 + FIRST : LEAD - 1 + I],
             func=ACT.Copy,
             scale=neg_pull[:],
         )
         faded = held.tile([P, T], F32, name="faded", tag="score_then_faded")
         nc.scalar.activation(out=faded[:], in_=old_sb[:], func=ACT.Copy, scale=fade_col[:])
 
-        for h in range(2):
-            nc.vector.tensor_tensor(
-                out=placed[:].indirect(own_list[:, entries[h]]),
-                in0=shares[:, LEAD + h * HALF : LEAD + (h + 1) * HALF],
-                in1=pulled[:, slots[h]],
-                op=ALU.add,
-            )
-            if h == 0:
-                nc.vector.tensor_scalar(
-                    out=total[:],
-                    in0=part_sum[0][:],
-                    scalar1=part_sum[1][:],
-                    scalar2=1.0 / 256.0,
-                    op0=ALU.add,
-                    op1=ALU.mult,
-                )
-        nc.vector.reciprocal(out=norm[:], in_=total[:])
+        nc.vector.tensor_copy(
+            out=placed[:].indirect(own_list[:, 0 : FIRST // 16]), in_=first_weights[:]
+        )
+        nc.vector.reciprocal(out=inverse[:], in_=total[:])
+        nc.vector.tensor_tensor(
+            out=placed[:].indirect(own_list[:, FIRST // 16 : I // 16]),
+            in0=shares[:, LEAD + FIRST : LEAD + I],
+            in1=pulled[:],
+            op=ALU.add,
+        )
+        nc.scalar.activation(out=norm[:], in_=inverse[:], func=ACT.Copy, scale=256.0)
 
-        for c in range(T // OUT_COLS):
-            cols = slice(c * OUT_COLS, (c + 1) * OUT_COLS)
-            result = held.tile([P, OUT_COLS], F32, name="result%d" % c)
+        for c, width in enumerate(OUT_WIDTHS):
+            cols = slice(sum(OUT_WIDTHS[:c]), sum(OUT_WIDTHS[: c + 1]))
+            result = held.tile([P, width], F32, name="result%d" % c)
             nc.vector.scalar_tensor_tensor(
                 out=result[:],
                 in0=placed[:, cols],

from contextlib import ExitStack

import concourse.mybir as mybir

D, T, I, Q = 512, 1024, 512, 128
FLOPS = 2 * D * T * Q

F32 = mybir.dt.float32
BF16 = mybir.dt.bfloat16
I32 = mybir.dt.int32
U32 = mybir.dt.uint32
U16 = mybir.dt.uint16
U8 = mybir.dt.uint8
FP8X4 = mybir.dt.float8_e4m3fn_x4
ALU = mybir.AluOpType
ACT = mybir.ActivationFunctionType

P = 128
PACK = 4
MM_WIDTHS = (256, 256, 256, 128, 128)
HALF = I // 2
LEAD = 8
FIRST = 128
OUT_WIDTHS = (256, 256, 256, 256)


def tile_attend_seconded_stepwise_counts_heads_kernel(
    tc, query, keys_words, keys_scales, lam, pull, old, fade, offs, offs2, offs3, out
):
    nc = tc.nc
    with ExitStack() as ctx:
        held = ctx.enter_context(tc.tile_pool(name="held", bufs=1))
        psum = ctx.enter_context(tc.psum_pool(name="psum", bufs=1))

        own_list = held.tile([P, I // 16], U16, name="own_list")
        seconder_list = held.tile([P, I // 16], U16, name="seconder_list")
        opponent_list = held.tile([P, I // 16], U16, name="opponent_list")

        key_scales = held.tile([P, T], U8, name="key_scales", align_bytes=64)

        q_raw = held.tile([P, PACK, Q], F32, name="q_raw")
        nc.sync.dma_start(out=q_raw[:], in_=query.rearrange("(p j) q -> p j q", j=PACK))
        for quad in range(4):
            queue = nc.sync if quad < 2 else nc.scalar
            queue.dma_start(
                out=key_scales[32 * quad : 32 * quad + 4, :].bitcast(I32),
                in_=keys_scales[0, 4 * quad : 4 * quad + 4, :].bitcast(I32),
            )
        key_words = held.tile([P, T], U32, name="key_words", align_bytes=64)
        words_hbm = keys_words[0].rearrange("p n t -> p (n t)").bitcast(I32)
        for c in range(2):
            cols = slice(c * T // 2, (c + 1) * T // 2)
            nc.sync.dma_start(out=key_words[:, cols].bitcast(I32), in_=words_hbm[:, cols])
        nc.sync.dma_start(opponent_list[:], offs3)
        nc.sync.dma_start(seconder_list[:], offs2)
        nc.sync.dma_start(own_list[:], offs)

        lam_col = held.tile([P, 1], F32, name="lam_col")
        pull_col = held.tile([P, 1], F32, name="pull_col")
        fade_col = held.tile([P, 1], F32, name="fade_col")
        nc.sync.dma_start(out=lam_col[:], in_=lam)
        nc.sync.dma_start(out=pull_col[:], in_=pull)
        nc.sync.dma_start(out=fade_col[:], in_=fade)
        old_sb = held.tile([P, T], F32, name="old_sb")
        nc.sync.dma_start(out=old_sb[:], in_=old)

        placed = held.tile([P, T], F32, name="placed")
        nc.vector.memset(placed[:], 0.0)
        shares = held.tile([P, LEAD + I], F32, name="shares")
        nc.vector.memset(shares[:, 0:LEAD], 0.0)

        q_grouped = held.tile([P, Q, PACK], BF16, name="q_grouped", align_bytes=64)
        q_halves = [slice(0, Q // 2), slice(Q // 2, Q)]
        for rows in q_halves:
            nc.vector.tensor_copy(
                out=q_grouped[:, rows, :], in_=q_raw[:, :, rows].rearrange("p j q -> p q j")
            )
        q_words = held.tile([P, Q], U32, name="q_words", align_bytes=64)
        q_scales = held.tile([P, Q], U8, name="q_scales", align_bytes=64)
        for rows in q_halves:
            nc.vector.quantize_mx(
                out=q_words[:, rows].bitcast(FP8X4),
                scales=q_scales[:, rows],
                in_=q_grouped[:, rows, :].rearrange("p q j -> p (q j)"),
            )

        neg_pull = held.tile([P, 1], F32, name="neg_pull")
        nc.gpsimd.tensor_scalar(
            out=neg_pull[:], in0=pull_col[:], scalar1=-1.0, scalar2=0.0, op0=ALU.mult, op1=ALU.add
        )

        products = held.tile([P, T], F32, name="products")
        for c, width in enumerate(MM_WIDTHS):
            cols = slice(sum(MM_WIDTHS[:c]), sum(MM_WIDTHS[: c + 1]))
            bank = psum.tile([P, width], F32, name="bank%d" % c)
            nc.tensor.matmul_mx(
                out=bank[:],
                lhsT=q_words[:].bitcast(FP8X4),
                lhsT_scale=q_scales[:],
                rhs=key_words[:, cols].bitcast(FP8X4),
                rhs_scale=key_scales[:, cols],
                start=True,
                stop=True,
            )
            if c % 2 == 0:
                nc.scalar.activation(out=products[:, cols], in_=bank[:], func=ACT.Copy)
            else:
                nc.vector.tensor_copy(out=products[:, cols], in_=bank[:])

        slots = [slice(0, HALF), slice(HALF, I)]
        entries = [slice(0, HALF // 16), slice(HALF // 16, I // 16)]

        opponent = held.tile([P, I], F32, name="opponent")
        seconder = [
            held.tile([P, HALF], F32, name="seconder0", tag="seconder_then_own"),
            held.tile([P, HALF], F32, name="seconder1"),
        ]
        gap = held.tile([P, I], F32, name="gap")
        vote = held.tile([P, I], F32, name="vote")
        score = held.tile([P, I], F32, name="score", tag="score_then_faded")
        neg_top = held.tile([P, 1], F32, name="neg_top")

        for h in range(2):
            nc.scalar.activation(
                out=opponent[:, slots[h]],
                in_=products[:].indirect(opponent_list[:, entries[h]]),
                func=ACT.Copy,
            )
            nc.vector.tensor_copy(
                out=seconder[h][:], in_=products[:].indirect(seconder_list[:, entries[h]])
            )
        for h in range(2):
            nc.vector.tensor_tensor(
                out=gap[:, slots[h]], in0=seconder[h][:], in1=opponent[:, slots[h]], op=ALU.subtract
            )
        own = [
            held.tile([P, HALF], F32, name="own0"),
            held.tile([P, HALF], F32, name="own1", tag="seconder_then_own"),
        ]
        nc.scalar.activation(
            out=own[0][:], in_=products[:].indirect(own_list[:, entries[0]]), func=ACT.Copy
        )
        nc.vector.tensor_copy(out=own[1][:], in_=products[:].indirect(own_list[:, entries[1]]))
        for h in range(2):
            nc.scalar.activation(out=vote[:, slots[h]], in_=gap[:, slots[h]], func=ACT.Tanh)
        for h in range(2):
            nc.vector.scalar_tensor_tensor(
                out=score[:, slots[h]],
                in0=vote[:, slots[h]],
                scalar=lam_col[:],
                in1=own[h][:],
                op0=ALU.mult,
                op1=ALU.add,
            )
        nc.vector.tensor_reduce(
            out=neg_top[:], in_=score[:], axis=mybir.AxisListType.X, op=ALU.max, negate=True
        )

        part_sum = [held.tile([P, 1], F32, name="part_sum%d" % h) for h in range(2)]
        pieces = [slice(0, FIRST), slice(FIRST, I)]
        for h in range(2):
            nc.scalar.activation(
                out=shares[:, LEAD + pieces[h].start : LEAD + pieces[h].stop],
                in_=score[:, pieces[h]],
                func=ACT.Exp,
                bias=neg_top[:],
                accum_out=part_sum[h][:],
            )
        first_weights = held.tile([P, FIRST], F32, name="first_weights")
        nc.vector.scalar_tensor_tensor(
            out=first_weights[:],
            in0=shares[:, LEAD - 1 : LEAD - 1 + FIRST],
            scalar=neg_pull[:],
            in1=shares[:, LEAD : LEAD + FIRST],
            op0=ALU.mult,
            op1=ALU.add,
        )
        total = held.tile([P, 1], F32, name="total")
        inverse = held.tile([P, 1], F32, name="inverse")
        norm = held.tile([P, 1], F32, name="norm")
        nc.scalar.activation(out=total[:], in_=part_sum[0][:], func=ACT.Identity, bias=part_sum[1][:])
        pulled = held.tile([P, I - FIRST], F32, name="pulled")
        nc.scalar.activation(
            out=pulled[:],
            in_=shares[:, LEAD - 1 + FIRST : LEAD - 1 + I],
            func=ACT.Copy,
            scale=neg_pull[:],
        )
        faded = held.tile([P, T], F32, name="faded", tag="score_then_faded")
        nc.scalar.activation(out=faded[:], in_=old_sb[:], func=ACT.Copy, scale=fade_col[:])

        nc.vector.tensor_copy(
            out=placed[:].indirect(own_list[:, 0 : FIRST // 16]), in_=first_weights[:]
        )
        nc.vector.reciprocal(out=inverse[:], in_=total[:])
        nc.vector.tensor_tensor(
            out=placed[:].indirect(own_list[:, FIRST // 16 : I // 16]),
            in0=shares[:, LEAD + FIRST : LEAD + I],
            in1=pulled[:],
            op=ALU.add,
        )
        nc.scalar.activation(out=norm[:], in_=inverse[:], func=ACT.Copy, scale=256.0)

        for c, width in enumerate(OUT_WIDTHS):
            cols = slice(sum(OUT_WIDTHS[:c]), sum(OUT_WIDTHS[: c + 1]))
            result = held.tile([P, width], F32, name="result%d" % c)
            nc.vector.scalar_tensor_tensor(
                out=result[:],
                in0=placed[:, cols],
                scalar=norm[:],
                in1=faded[:, cols],
                op0=ALU.mult,
                op1=ALU.add,
            )
            queue = nc.sync if c % 2 == 0 else nc.scalar
            queue.dma_start(out=out[:, cols], in_=result[:])
